import numpy as np
import ml_dtypes


def mxq(x, axis, fmt="e4m3"):
    dtype, down = {"e4m3": (ml_dtypes.float8_e4m3fn, 7), "e5m2": (ml_dtypes.float8_e5m2, 14)}[fmt]
    v = np.moveaxis(np.asarray(x, np.float32).astype(ml_dtypes.bfloat16).astype(np.float64), axis, -1)
    blocks = v.reshape(v.shape[:-1] + (-1, 32))
    amax = np.abs(blocks).max(-1, keepdims=True)
    byte = np.maximum(np.where(amax > 0, np.frexp(amax)[1] - 1 + 127, 0) - down, 1)
    scale = np.exp2(byte - 127.0)
    codes = (blocks / scale).astype(np.float32).astype(dtype).astype(np.float64)
    return np.moveaxis((codes * scale).reshape(v.shape), -1, axis)


WIDE = False


def mx_kscale(k):
    if not WIDE:
        return np.ones(k)
    levels = np.array([10, -10, 5, -5, 0])
    if k % 512:
        return np.exp2(np.random.permutation(np.resize(levels, k // 32))).repeat(32)
    a = np.empty((k // 512, 16))
    for p in range(k // 512):
        a[p, :8] = np.random.permutation(np.resize(levels, 8))
        for g in range(8):
            far = levels[np.abs(levels - a[p, g]) >= 10]
            a[p, g + 8] = far[np.random.randint(len(far))]
    return np.exp2(a.ravel()).repeat(32)


def f64(x):
    return np.asarray(x).astype(np.float64)


def striped(idx):
    return np.tile(idx.reshape(-1, 16).T, (8, 1)).astype(np.uint16)


def unstriped(offs):
    return offs[:16].T.reshape(-1).astype(np.int64)


def pack_weight(w):
    k, n = w.shape
    w = f64(np.asarray(w, np.float32).astype(ml_dtypes.bfloat16)).reshape(k // 32, 32, n)
    amax = np.abs(w).max(1)
    byte = np.clip(np.where(amax > 0, np.frexp(amax)[1] - 1 + 127 - 7, 1), 1, 254)
    scaled = (w * np.exp2(127.0 - byte)[:, None, :]).reshape(k, n).astype(np.float32)
    words = np.ascontiguousarray(scaled.reshape(k // 512, 128, 4, n).transpose(0, 1, 3, 2)).astype(ml_dtypes.float8_e4m3fn).view(np.uint8)
    return words, np.ascontiguousarray(byte.astype(np.uint8).reshape(k // 512, 16, n))


def unpack_weight(words, scales):
    g, p, n, _ = words.shape
    vals = np.ascontiguousarray(words).view(ml_dtypes.float8_e4m3fn).astype(np.float64) * np.repeat(np.exp2(scales.astype(np.float64) - 127.0), 8, axis=1)[..., None]
    return vals.transpose(0, 1, 3, 2).reshape(g * 512, n)


E2M1 = np.array([0.0, 0.5, 1.0, 1.5, 2.0, 3.0, 4.0, 6.0, -0.0, -0.5, -1.0, -1.5, -2.0, -3.0, -4.0, -6.0])


def pack_fp4(w):
    k, n = w.shape
    w = f64(np.asarray(w, np.float32).astype(ml_dtypes.bfloat16)).reshape(k // 32, 32, n)
    amax = np.abs(w).max(1)
    mant, ex = np.frexp(amax / 6.0)
    byte = np.clip(np.where(amax > 0, np.where(mant > 0.5, ex, ex - 1) + 127, 1), 1, 254)
    scaled = (w * np.exp2(127.0 - byte)[:, None, :]).reshape(k, n).astype(np.float32)
    c = np.ascontiguousarray(scaled.reshape(k // 512, 128, 4, n).transpose(0, 1, 3, 2)).astype(ml_dtypes.float4_e2m1fn).view(np.uint8) & 0xF
    words = (c[..., 0::2] | (c[..., 1::2] << 4)).reshape(k // 512, 128, 2 * n)
    return np.ascontiguousarray(words), np.ascontiguousarray(byte.astype(np.uint8).reshape(k // 512, 16, n))


def unpack_fp4(words, scales):
    g, _, n = scales.shape
    words = np.ascontiguousarray(words).reshape(g, 128, n, 2)
    nib = np.empty((g, 128, n, 4), np.uint8)
    nib[..., 0::2] = words & 0xF
    nib[..., 1::2] = words >> 4
    vals = E2M1[nib] * np.repeat(np.exp2(scales.astype(np.float64) - 127.0), 8, axis=1)[..., None]
    return vals.transpose(0, 1, 3, 2).reshape(g * 512, n)


def sigmoid(v):
    return 1.0 / (1.0 + np.exp(-np.maximum(v, -700.0)))


K, T, S, D, N, H, V, U = 512, 2048, 1024, 4, 128, 512, 256, 512


def setup_inputs():
    n = np.random.standard_normal
    s = mx_kscale(K)[:, None]
    u = mx_kscale(H)
    packed_xT = pack_weight(n((K, T)) * s)
    packed_w1 = pack_fp4(n((K, H)) / np.sqrt(K) / s)
    packed_w2 = pack_fp4(n((K, H)) / np.sqrt(K) / s)
    packed_w3 = pack_fp4(n((H, N)) / np.sqrt(H) / u[:, None])
    return {
        "x_words": packed_xT[0],
        "x_scales": packed_xT[1],
        "w1_words": packed_w1[0],
        "w1_scales": packed_w1[1],
        "w2_words": packed_w2[0],
        "w2_scales": packed_w2[1],
        "ref": (np.random.uniform(0.5, 2.5, (H, S))).astype(np.float32),
        "unit": (np.random.uniform(0.6, 1.4, (H, 1)) * u[:, None]).astype(np.float32),
        "w3_words": packed_w3[0],
        "w3_scales": packed_w3[1],
        "offs": striped(np.random.permutation(T)[:S]),
        "par": striped(np.random.permutation(S)),
        "dom": striped(np.random.permutation(np.concatenate([np.arange(V), np.random.randint(0, V, U - V)]))),
    }


def reference(x_words, x_scales, w1_words, w1_scales, w2_words, w2_scales, ref, unit, w3_words, w3_scales, offs, par, dom):
    xq = unpack_weight(x_words, x_scales)[:, unstriped(offs)]
    px = unpack_fp4(w1_words, w1_scales).T @ xq
    xp = px[:, unstriped(par)]
    py = unpack_fp4(w2_words, w2_scales).T @ xq
    yp = py[:, unstriped(par)]
    dis = np.sqrt((px - xp) ** 2 + (py - yp) ** 2 + 0.05)
    err = np.abs(dis - f64(ref))
    s1 = sigmoid(-4.0 * err + 2.0)
    s2 = sigmoid(-4.0 * err + 5.0)
    sc = 0.5 * (s1 + s2)
    lddt = sc.reshape(len(sc), -1, D).mean(axis=2)
    md = lddt[:, unstriped(dom)]
    worst = err.reshape(len(err), -1, D).max(axis=2)
    wd = worst[:, unstriped(dom)]
    hid = f64(unit) * (md - wd)
    return unpack_fp4(w3_words, w3_scales).T @ mxq(hid, 0, "e4m3")

@@ -1,0 +1,298 @@
+from contextlib import ExitStack
+
+import concourse.mybir as mybir
+from concourse.masks import make_identity
+
+K, T, S, D, N, H, V, U = 512, 2048, 1024, 4, 128, 512, 256, 512
+FLOPS = 2 * (2 * K * H * S + H * N * U)
+
+F32 = mybir.dt.float32
+BF16 = mybir.dt.bfloat16
+I32 = mybir.dt.int32
+U32 = mybir.dt.uint32
+U16 = mybir.dt.uint16
+U8 = mybir.dt.uint8
+FP8X4 = mybir.dt.float8_e4m3fn_x4
+FP4X4 = mybir.dt.float4_e2m1fn_x4
+ALU = mybir.AluOpType
+ACT = mybir.ActivationFunctionType
+AXIS = mybir.AxisListType
+
+P = 128
+PACK = 4
+BANK = 512
+LANES = 16
+LAST = PACK - 1
+AHEAD = 2
+NEG = "VAAA"
+HALVED = (3,)
+VECTOR_COPIES = ()
+UNFUSED = ((0, 0),)
+SCALAR_GATHERS = ()
+DOM = "VVVVVVVA"
+QE = "VVVV"
+
+
+def load_scale_rows(queue, plane, scales):
+    for q in range(4):
+        queue.dma_start(
+            out=plane[32 * q : 32 * q + 4, :].bitcast(I32),
+            in_=scales[0, 4 * q : 4 * q + 4, :].bitcast(I32),
+        )
+
+
+def tile_picked_ylddts_worst_p_kernel(
+    tc, x_words, x_scales, w1_words, w1_scales, w2_words, w2_scales, ref, unit,
+    w3_words, w3_scales, offs, par, dom, out,
+):
+    nc = tc.nc
+    with ExitStack() as ctx:
+        keep = ctx.enter_context(tc.tile_pool(name="keep", bufs=1))
+        coords = ctx.enter_context(tc.tile_pool(name="coords", bufs=2))
+        twins = ctx.enter_context(tc.tile_pool(name="twins", bufs=2))
+        works = ctx.enter_context(tc.tile_pool(name="works", bufs=3))
+        ring = ctx.enter_context(tc.tile_pool(name="ring", bufs=2))
+        mm_pool = ctx.enter_context(tc.psum_pool(name="mm", bufs=4))
+        err_pool = ctx.enter_context(tc.psum_pool(name="errs", bufs=2))
+        sum_pool = ctx.enter_context(tc.psum_pool(name="sums", bufs=2))
+
+        def held(name, shape, dtype, tag=None):
+            return keep.tile(shape, dtype, name=name, tag=tag or name, align_bytes=64)
+
+        offs_sb = held("offs_sb", [P, S // LANES], U16)
+        par_sb = held("par_sb", [P, S // LANES], U16)
+        dom_sb = held("dom_sb", [P, U // LANES], U16)
+        x_table = held("x_table", [P, T], I32)
+        x_plane = held("x_plane", [P, T], U8)
+        w_raw = [held("w_raw%d" % c, [P, 2 * H], U8) for c in range(2)]
+        w_plane_raw = [held("w_plane_raw%d" % c, [P, H], U8) for c in range(2)]
+        ident = held("ident", [P, P], F32)
+
+        nc.gpsimd.memset(x_plane[:].bitcast(I32), 0)
+        for plane in w_plane_raw:
+            nc.gpsimd.memset(plane[:].bitcast(I32), 0)
+
+        load_scale_rows(nc.scalar, x_plane[:], x_scales)
+        nc.sync.dma_start(out=offs_sb[:], in_=offs)
+        nc.sync.dma_start(out=par_sb[:], in_=par)
+        nc.sync.dma_start(out=dom_sb[:], in_=dom)
+        nc.sync.dma_start(out=x_table[:], in_=x_words[0].rearrange("p n r -> p (n r)").bitcast(I32))
+        nc.gpsimd.dma_start(out=w_raw[0][:].bitcast(I32), in_=w1_words[0].bitcast(I32))
+        nc.gpsimd.dma_start(out=w_raw[1][:].bitcast(I32), in_=w2_words[0].bitcast(I32))
+        load_scale_rows(nc.sync, w_plane_raw[0][:], w1_scales)
+        load_scale_rows(nc.scalar, w_plane_raw[1][:], w2_scales)
+        unit_sb = held("unit_sb", [P, PACK], F32)
+        w3_sb = held("w3_sb", [P, 2 * N], U8)
+        w3_plane = held("w3_plane", [P, N], U8)
+        make_identity(nc, ident[:])
+        nc.gpsimd.memset(w3_plane[:].bitcast(I32), 0)
+        nc.gpsimd.dma_start(out=unit_sb[:], in_=unit.rearrange("(p t) o -> p (t o)", t=PACK))
+        nc.gpsimd.dma_start(out=w3_sb[:].bitcast(I32), in_=w3_words[0].bitcast(I32))
+        load_scale_rows(nc.gpsimd, w3_plane[:], w3_scales)
+
+        w_sb = [held("w_sb%d" % c, [P, 2 * H], U8) for c in range(2)]
+        w_plane = [held("w_plane%d" % c, [P, H], U8) for c in range(2)]
+        xq_plane = [held("xq_plane%d" % h, [P, BANK], U8) for h in range(2)]
+        step = BANK // LANES
+        for c in range(2):
+            nc.scalar.copy(
+                out=w_sb[c][:].bitcast(U16).rearrange("p (t m) -> p t m", t=PACK),
+                in_=w_raw[c][:].bitcast(U16).rearrange("p (m t) -> p t m", t=PACK),
+            )
+
+        def deal_plane(c):
+            nc.vector.tensor_copy(
+                out=w_plane[c][:].rearrange("p (t m) -> p t m", t=PACK),
+                in_=w_plane_raw[c][:].rearrange("p (m t) -> p t m", t=PACK),
+            )
+
+        deal_plane(0)
+        for h in range(2):
+            nc.vector.tensor_copy(out=xq_plane[h][:], in_=x_plane[:].indirect(offs_sb[:, h * step : (h + 1) * step]))
+        xq_words = [held("xq_words0", [P, BANK], U32), held("xq_words1", [P, BANK], U32, tag="w_plane_raw0")]
+        for h in range(2):
+            nc.vector.tensor_copy(
+                out=xq_words[h][:], in_=x_table[:].bitcast(U32).indirect(offs_sb[:, h * step : (h + 1) * step])
+            )
+        deal_plane(1)
+
+        ref_late = held("ref_late", [P, 2, S], F32, tag="x_table")
+        ref_sb = [held("ref%d" % c, [P, S], F32, tag="w_raw%d" % c)[:] for c in range(2)] + [ref_late[:, c, :] for c in range(2)]
+        ref_rows = ref.rearrange("(p t) j -> p t j", t=PACK)
+        for t in range(PACK):
+            nc.sync.dma_start(out=ref_sb[t], in_=ref_rows[:, t, :])
+        unit_scale = held("unit_scale", [P, PACK], F32)
+        unit_bias = held("unit_bias", [P, PACK], F32)
+        nc.gpsimd.tensor_scalar(unit_scale[:], unit_sb[:], -1.0 / 16.0, 0.0, ALU.mult, ALU.add)
+        nc.gpsimd.tensor_scalar(unit_bias[:], unit_sb[:], 0.5, 0.0, ALU.mult, ALU.add)
+
+        err = [held("err%d" % t, [P, 2, D, P], F32) for t in range(PACK)]
+        worst = [held("worst%d" % t, [P, 2, P], F32) for t in range(PACK)]
+        planes = [held("planes%d" % h, [P, PACK, U // 2], BF16) for h in range(2)]
+        coord, twin, work, square, minus_ref = {}, {}, {}, {}, {}
+
+        def project(t):
+            for c in range(2):
+                coord[t, c] = coords.tile([P, S], F32, name="coord%d" % c)
+                for h in range(2):
+                    acc = mm_pool.tile([P, BANK], F32, name="acc")
+                    nc.tensor.matmul_mx(
+                        out=acc[:],
+                        lhsT=w_sb[c][:, 2 * P * t : 2 * P * (t + 1)].bitcast(FP4X4),
+                        lhsT_scale=w_plane[c][:, P * t : P * (t + 1)],
+                        rhs=xq_words[h][:].bitcast(FP8X4),
+                        rhs_scale=xq_plane[h][:],
+                        start=True,
+                        stop=True,
+                    )
+                    into = coord[t, c][:, h * BANK : (h + 1) * BANK]
+                    if (t, c, h) in VECTOR_COPIES:
+                        nc.vector.tensor_copy(out=into, in_=acc[:])
+                    else:
+                        nc.scalar.copy(out=into, in_=acc[:])
+                if (t, c) not in UNFUSED:
+                    twin[t, c] = twins.tile([P, S], F32, name="twin%d" % c)
+                    nc.sync.dma_start(out=twin[t, c][:], in_=coord[t, c][:])
+
+        def differences(t, h):
+            cols = slice(h * BANK, (h + 1) * BANK)
+            work[t, h] = works.tile([P, 2, BANK], F32, name="work")
+            for c in range(2):
+                partner = coord[t, c][:].indirect(par_sb[:, h * step : (h + 1) * step])
+                into = work[t, h][:, c, :]
+                if (t, c) not in UNFUSED:
+                    nc.vector.tensor_tensor(out=into, in0=partner, in1=twin[t, c][:, cols], op=ALU.subtract)
+                    continue
+                if (t, c) in SCALAR_GATHERS:
+                    nc.scalar.activation(out=into, in_=partner, func=ACT.Copy)
+                else:
+                    nc.vector.tensor_copy(out=into, in_=partner)
+                nc.vector.tensor_tensor(out=into, in0=into, in1=coord[t, c][:, cols], op=ALU.subtract)
+            nc.scalar.activation(out=work[t, h][:], in_=work[t, h][:], func=ACT.Square)
+
+        def negate(t, h):
+            minus_ref[t, h] = ring.tile([P, D, P], F32, name="minus_ref")
+            into = minus_ref[t, h][:].rearrange("p d v -> p v d")
+            source = ref_sb[t][:, h * BANK : (h + 1) * BANK].rearrange("p (v d) -> p v d", d=D)
+            if NEG[t] == "A":
+                nc.scalar.activation(out=into, in_=source, func=ACT.Copy, scale=-16.0)
+            else:
+                nc.vector.tensor_scalar(into, source, -16.0, None, ALU.mult)
+
+        def distance(t, h):
+            square[t, h] = ring.tile([P, BANK], F32, name="square")
+            nc.vector.tensor_tensor(out=square[t, h][:], in0=work[t, h][:, 0, :], in1=work[t, h][:, 1, :], op=ALU.add)
+            dis = ring.tile([P, D, P], F32, name="dis")
+            nc.scalar.activation(
+                out=dis[:].rearrange("p d v -> p v d"), in_=square[t, h][:].rearrange("p (v d) -> p v d", d=D),
+                func=ACT.Sqrt, scale=256.0, bias=256.0 * 0.05,
+            )
+            signed = err_pool.tile([P, D, P], F32, name="signed")
+            for n, term in enumerate((minus_ref[t, h], dis)):
+                for d in range(D):
+                    nc.tensor.matmul(
+                        out=signed[:, d, :], lhsT=term[:, d, :], rhs=ident[:], is_transpose=True,
+                        start=(n == 0 and d == 0), stop=(n == 1 and d == D - 1),
+                    )
+            return signed
+
+        def largest(t):
+            pairs = ring.tile([P, 2, 2, P], F32, name="pairs")
+            nc.vector.tensor_tensor(out=pairs[:], in0=err[t][:, :, 0:2, :], in1=err[t][:, :, 2:4, :], op=ALU.max)
+            nc.vector.tensor_tensor(out=worst[t][:], in0=pairs[:, :, 0, :], in1=pairs[:, :, 1, :], op=ALU.max)
+
+        units = [(t, h) for t in range(PACK) for h in range(2)]
+        signed = {}
+        for t in range(AHEAD):
+            project(t)
+        for n in range(len(units) + 2):
+            if n < len(units):
+                differences(*units[n])
+                t, h = units[n]
+                if h == 1 and t + AHEAD < PACK:
+                    project(t + AHEAD)
+            if 0 <= n < len(units) + 0:
+                negate(*units[n - 0])
+            if 1 <= n < len(units) + 1:
+                signed[units[n - 1]] = distance(*units[n - 1])
+            if n >= 2:
+                t, h = units[n - 2]
+                nc.scalar.activation(out=err[t][:, h, :, :], in_=signed[t, h][:], func=ACT.Abs)
+                if h == 1 and t < 8:
+                    largest(t)
+        for t in range(8, PACK):
+            largest(t)
+
+        shifts = square[LAST, 1][:, BANK - 2 :]
+        nc.gpsimd.memset(shifts[:, 0:1], -1.0)
+        nc.gpsimd.memset(shifts[:, 1:2], -2.5)
+
+        def score(t):
+            soft = held("soft%d" % t, [P, 2, 2, D, P], F32)
+            for part in ([slice(0, 1), slice(1, 2)] if t in HALVED else [slice(0, 2)]):
+                for s in range(2):
+                    nc.scalar.activation(
+                        out=soft[:, s, part, :, :], in_=err[t][:, part, :, :], func=ACT.Tanh,
+                        scale=0.125, bias=shifts[:, s : s + 1],
+                    )
+            total = sum_pool.tile([P, V], F32, name="total")
+            if t in HALVED:
+                order = [(n, h) for h in range(2) for n in range(2 * D + 1)]
+            else:
+                order = [(n, h) for n in range(2 * D + 1) for h in range(2)]
+            for n, h in order:
+                term = worst[t][:, h, :] if n == 0 else soft[:, (n - 1) // D, h, (n - 1) % D, :]
+                nc.tensor.matmul(
+                    out=total[:, h * P : (h + 1) * P], lhsT=term, rhs=ident[:],
+                    is_transpose=True, start=((n, h) == order[0]), stop=((n, h) == order[-1]),
+                )
+            value = err[t][:].rearrange("p h d v -> p (h d v)")[:, :V]
+            if QE[t] == "V":
+                nc.vector.tensor_scalar(
+                    value, total[:], unit_scale[:, t : t + 1], unit_bias[:, t : t + 1], ALU.mult, ALU.add
+                )
+            else:
+                nc.scalar.activation(
+                    out=value, in_=total[:], func=ACT.Identity,
+                    scale=unit_scale[:, t : t + 1], bias=unit_bias[:, t : t + 1],
+                )
+
+        slot_step = U // 2 // LANES
+
+        def look_up(t):
+            for h in range(2):
+                value = err[t][:].rearrange("p h d v -> p (h d v)").indirect(dom_sb[:, h * slot_step : (h + 1) * slot_step])
+                if DOM[2 * t + h] == "A":
+                    nc.scalar.activation(out=planes[h][:, t, :], in_=value, func=ACT.Copy)
+                else:
+                    nc.vector.tensor_copy(out=planes[h][:, t, :], in_=value)
+
+        for t in range(PACK):
+            score(t)
+        for t in range(PACK):
+            look_up(t)
+
+        for h in range(2):
+            hid = held("hid%d" % h, [P, U // 2, PACK], BF16)
+            codes = held("codes%d" % h, [P, U // 2], U32)
+            hid_plane = held("hid_plane%d" % h, [P, U // 2], U8)
+            result = held("result%d" % h, [P, U // 2], F32)
+            nc.vector.tensor_copy(
+                out=hid[:].rearrange("p (c i) t -> p c t i", i=4),
+                in_=planes[h][:].rearrange("p t (c i) -> p c t i", i=4),
+            )
+            nc.vector.quantize_mx(
+                out=codes[:].bitcast(FP8X4), scales=hid_plane[:], in_=hid[:].rearrange("p r t -> p (r t)")
+            )
+            acc = mm_pool.tile([P, BANK], F32, name="acc")
+            nc.tensor.matmul_mx(
+                out=acc[:, : U // 2],
+                lhsT=w3_sb[:].bitcast(FP4X4),
+                lhsT_scale=w3_plane[:],
+                rhs=codes[:].bitcast(FP8X4),
+                rhs_scale=hid_plane[:],
+                start=True,
+                stop=True,
+            )
+            nc.scalar.copy(out=result[:], in_=acc[:, : U // 2])
+            nc.sync.dma_start(out=out[:, h * (U // 2) : (h + 1) * (U // 2)], in_=result[:])

@@ -16,29 +16,29 @@ FP8X4 = mybir.dt.float8_e4m3fn_x4
 FP4X4 = mybir.dt.float4_e2m1fn_x4
 ALU = mybir.AluOpType
 ACT = mybir.ActivationFunctionType
-AXIS = mybir.AxisListType
 
 P = 128
 PACK = 4
 BANK = 512
 LANES = 16
-LAST = PACK - 1
-AHEAD = 2
-NEG = "VAAA"
-HALVED = (3,)
-VECTOR_COPIES = ()
-UNFUSED = ((0, 0),)
-SCALAR_GATHERS = ()
-DOM = "VVVVVVVA"
-QE = "VVVV"
+RUN = P // PACK
+TERMS = 2 * D
+PIECES = [(t, h) for t in range(PACK) for h in range(2)]
+LAST = len(PIECES) - 1
+VECTOR_COPIES = 3
+PRE_ADDED = 5
 
 
-def load_scale_rows(queue, plane, scales):
+def load_scale_rows(nc, plane, scales):
     for q in range(4):
-        queue.dma_start(
+        nc.sync.dma_start(
             out=plane[32 * q : 32 * q + 4, :].bitcast(I32),
             in_=scales[0, 4 * q : 4 * q + 4, :].bitcast(I32),
         )
+
+
+def on_tensor(n):
+    return n % 2 == 1 and n != LAST
 
 
 def tile_picked_ylddts_worst_p_kernel(
@@ -48,251 +48,304 @@ def tile_picked_ylddts_worst_p_kernel(
     nc = tc.nc
     with ExitStack() as ctx:
         keep = ctx.enter_context(tc.tile_pool(name="keep", bufs=1))
-        coords = ctx.enter_context(tc.tile_pool(name="coords", bufs=2))
-        twins = ctx.enter_context(tc.tile_pool(name="twins", bufs=2))
-        works = ctx.enter_context(tc.tile_pool(name="works", bufs=3))
-        ring = ctx.enter_context(tc.tile_pool(name="ring", bufs=2))
-        mm_pool = ctx.enter_context(tc.psum_pool(name="mm", bufs=4))
-        err_pool = ctx.enter_context(tc.psum_pool(name="errs", bufs=2))
-        sum_pool = ctx.enter_context(tc.psum_pool(name="sums", bufs=2))
+        psum = ctx.enter_context(tc.psum_pool(name="psum", bufs=1))
 
-        def held(name, shape, dtype, tag=None):
-            return keep.tile(shape, dtype, name=name, tag=tag or name, align_bytes=64)
+        def held(name, shape, dtype):
+            return keep.tile(shape, dtype, name=name, align_bytes=64)
+
+        banks = [psum.tile([P, BANK], F32, name="bank%d" % b) for b in range(8)]
+        roles = {
+            "first": banks, "difference": banks[0:2], "product": banks[2:4], "square": banks[4:6],
+            "signed": banks[6:8], "score": banks[0:4],
+        }
+        uses = {role: 0 for role in roles}
+
+        def next_bank(role):
+            uses[role] += 1
+            return roles[role][(uses[role] - 1) % len(roles[role])]
 
         offs_sb = held("offs_sb", [P, S // LANES], U16)
         par_sb = held("par_sb", [P, S // LANES], U16)
         dom_sb = held("dom_sb", [P, U // LANES], U16)
-        x_table = held("x_table", [P, T], I32)
         x_plane = held("x_plane", [P, T], U8)
-        w_raw = [held("w_raw%d" % c, [P, 2 * H], U8) for c in range(2)]
-        w_plane_raw = [held("w_plane_raw%d" % c, [P, H], U8) for c in range(2)]
+        x_table = held("x_table", [P, T], I32)
+        w_sb = [held("w_sb%d" % c, [P, 2 * H], U8) for c in range(2)]
+        w_plane = [held("w_plane%d" % c, [P, H], U8) for c in range(2)]
         ident = held("ident", [P, P], F32)
 
-        nc.gpsimd.memset(x_plane[:].bitcast(I32), 0)
-        for plane in w_plane_raw:
-            nc.gpsimd.memset(plane[:].bitcast(I32), 0)
+        window = {(t, c): held("window%d_%d" % (t, c), [P, 2 * S], F32) for t in range(PACK) for c in range(2)}
+        ref_sb = [window[t // 2, t % 2][:, S:] for t in range(PACK)]
+        minus_ref = [window[2 + t // 2, t % 2][:, S:] for t in range(PACK)]
 
-        load_scale_rows(nc.scalar, x_plane[:], x_scales)
+        def load_ref(t):
+            nc.sync.dma_start(out=ref_sb[t], in_=ref[P * t : P * (t + 1), :])
+
+        nc.gpsimd.memset(x_plane[:, : T // 2].bitcast(I32), 0)
+        nc.vector.memset(x_plane[:, T // 2 :].bitcast(I32), 0)
+        for plane in w_plane:
+            nc.vector.memset(plane[:].bitcast(I32), 0)
+
         nc.sync.dma_start(out=offs_sb[:], in_=offs)
         nc.sync.dma_start(out=par_sb[:], in_=par)
-        nc.sync.dma_start(out=dom_sb[:], in_=dom)
+        load_scale_rows(nc, x_plane[:], x_scales)
         nc.sync.dma_start(out=x_table[:], in_=x_words[0].rearrange("p n r -> p (n r)").bitcast(I32))
-        nc.gpsimd.dma_start(out=w_raw[0][:].bitcast(I32), in_=w1_words[0].bitcast(I32))
-        nc.gpsimd.dma_start(out=w_raw[1][:].bitcast(I32), in_=w2_words[0].bitcast(I32))
-        load_scale_rows(nc.sync, w_plane_raw[0][:], w1_scales)
-        load_scale_rows(nc.scalar, w_plane_raw[1][:], w2_scales)
+        nc.gpsimd.dma_start(out=w_sb[0][:].bitcast(I32), in_=w1_words[0].bitcast(I32))
+        nc.gpsimd.dma_start(out=w_sb[1][:].bitcast(I32), in_=w2_words[0].bitcast(I32))
+        load_ref(0)
+        load_scale_rows(nc, w_plane[0][:], w1_scales)
+        load_scale_rows(nc, w_plane[1][:], w2_scales)
+        for t in range(1, PACK):
+            load_ref(t)
+        nc.sync.dma_start(out=dom_sb[:], in_=dom)
+        make_identity(nc, ident[:])
         unit_sb = held("unit_sb", [P, PACK], F32)
         w3_sb = held("w3_sb", [P, 2 * N], U8)
         w3_plane = held("w3_plane", [P, N], U8)
-        make_identity(nc, ident[:])
-        nc.gpsimd.memset(w3_plane[:].bitcast(I32), 0)
-        nc.gpsimd.dma_start(out=unit_sb[:], in_=unit.rearrange("(p t) o -> p (t o)", t=PACK))
-        nc.gpsimd.dma_start(out=w3_sb[:].bitcast(I32), in_=w3_words[0].bitcast(I32))
-        load_scale_rows(nc.gpsimd, w3_plane[:], w3_scales)
+        nc.vector.memset(w3_plane[:].bitcast(I32), 0)
+        nc.sync.dma_start(out=unit_sb[:], in_=unit.rearrange("(p r) o -> p (r o)", r=PACK))
+        nc.sync.dma_start(out=w3_sb[:].bitcast(I32), in_=w3_words[0].bitcast(I32))
+        load_scale_rows(nc, w3_plane[:], w3_scales)
 
-        w_sb = [held("w_sb%d" % c, [P, 2 * H], U8) for c in range(2)]
-        w_plane = [held("w_plane%d" % c, [P, H], U8) for c in range(2)]
+        def entries(list_sb, lo, hi):
+            return list_sb[:, lo // LANES : hi // LANES]
+
         xq_plane = [held("xq_plane%d" % h, [P, BANK], U8) for h in range(2)]
-        step = BANK // LANES
-        for c in range(2):
-            nc.scalar.copy(
-                out=w_sb[c][:].bitcast(U16).rearrange("p (t m) -> p t m", t=PACK),
-                in_=w_raw[c][:].bitcast(U16).rearrange("p (m t) -> p t m", t=PACK),
-            )
-
-        def deal_plane(c):
-            nc.vector.tensor_copy(
-                out=w_plane[c][:].rearrange("p (t m) -> p t m", t=PACK),
-                in_=w_plane_raw[c][:].rearrange("p (m t) -> p t m", t=PACK),
-            )
-
-        deal_plane(0)
+        xq_words = [held("xq_words%d" % h, [P, BANK], U32) for h in range(2)]
+        quarters = ((0, BANK // 2), (BANK // 2, BANK))
         for h in range(2):
-            nc.vector.tensor_copy(out=xq_plane[h][:], in_=x_plane[:].indirect(offs_sb[:, h * step : (h + 1) * step]))
-        xq_words = [held("xq_words0", [P, BANK], U32), held("xq_words1", [P, BANK], U32, tag="w_plane_raw0")]
-        for h in range(2):
-            nc.vector.tensor_copy(
-                out=xq_words[h][:], in_=x_table[:].bitcast(U32).indirect(offs_sb[:, h * step : (h + 1) * step])
-            )
-        deal_plane(1)
+            picks = entries(offs_sb, h * BANK, (h + 1) * BANK)
+            nc.vector.tensor_copy(out=xq_plane[h][:], in_=x_plane[:].indirect(picks))
+        words = x_table[:].bitcast(U32)
+        nc.vector.tensor_copy(out=xq_words[0][:], in_=words.indirect(entries(offs_sb, 0, BANK)))
+        for lo, hi in quarters:
+            nc.vector.tensor_copy(out=xq_words[1][:, lo:hi], in_=words.indirect(entries(offs_sb, BANK + lo, BANK + hi)))
 
-        ref_late = held("ref_late", [P, 2, S], F32, tag="x_table")
-        ref_sb = [held("ref%d" % c, [P, S], F32, tag="w_raw%d" % c)[:] for c in range(2)] + [ref_late[:, c, :] for c in range(2)]
-        ref_rows = ref.rearrange("(p t) j -> p t j", t=PACK)
-        for t in range(PACK):
-            nc.sync.dma_start(out=ref_sb[t], in_=ref_rows[:, t, :])
         unit_scale = held("unit_scale", [P, PACK], F32)
         unit_bias = held("unit_bias", [P, PACK], F32)
-        nc.gpsimd.tensor_scalar(unit_scale[:], unit_sb[:], -1.0 / 16.0, 0.0, ALU.mult, ALU.add)
+        nc.gpsimd.tensor_scalar(unit_scale[:], unit_sb[:], -1.0 / (2 * TERMS), 0.0, ALU.mult, ALU.add)
         nc.gpsimd.tensor_scalar(unit_bias[:], unit_sb[:], 0.5, 0.0, ALU.mult, ALU.add)
 
-        err = [held("err%d" % t, [P, 2, D, P], F32) for t in range(PACK)]
-        worst = [held("worst%d" % t, [P, 2, P], F32) for t in range(PACK)]
-        planes = [held("planes%d" % h, [P, PACK, U // 2], BF16) for h in range(2)]
-        coord, twin, work, square, minus_ref = {}, {}, {}, {}, {}
+        err16 = held("err16", [P, PACK, 2, D, P], F32)
+        worst16 = [held("worst16_%d" % h, [P, PACK, P], F32) for h in range(2)]
+        partners = [held("partner%d" % b, [P, 2, BANK], F32) for b in range(2)]
+        squares = [held("square%d" % b, [P, 2, BANK], F32) for b in range(2)]
+        distances = [held("distance%d" % b, [P, BANK], F32) for b in range(2)]
+        last_gap = held("last_gap", [P, BANK], F32)
+        pairs = [held("pairs%d" % h, [P, PACK, 2, P], F32) for h in range(2)]
+        difference, square_sum, signed = {}, {}, {}
 
-        def project(t):
-            for c in range(2):
-                coord[t, c] = coords.tile([P, S], F32, name="coord%d" % c)
-                for h in range(2):
-                    acc = mm_pool.tile([P, BANK], F32, name="acc")
-                    nc.tensor.matmul_mx(
-                        out=acc[:],
-                        lhsT=w_sb[c][:, 2 * P * t : 2 * P * (t + 1)].bitcast(FP4X4),
-                        lhsT_scale=w_plane[c][:, P * t : P * (t + 1)],
-                        rhs=xq_words[h][:].bitcast(FP8X4),
-                        rhs_scale=xq_plane[h][:],
-                        start=True,
-                        stop=True,
-                    )
-                    into = coord[t, c][:, h * BANK : (h + 1) * BANK]
-                    if (t, c, h) in VECTOR_COPIES:
-                        nc.vector.tensor_copy(out=into, in_=acc[:])
-                    else:
-                        nc.scalar.copy(out=into, in_=acc[:])
-                if (t, c) not in UNFUSED:
-                    twin[t, c] = twins.tile([P, S], F32, name="twin%d" % c)
-                    nc.sync.dma_start(out=twin[t, c][:], in_=coord[t, c][:])
-
-        def differences(t, h):
-            cols = slice(h * BANK, (h + 1) * BANK)
-            work[t, h] = works.tile([P, 2, BANK], F32, name="work")
-            for c in range(2):
-                partner = coord[t, c][:].indirect(par_sb[:, h * step : (h + 1) * step])
-                into = work[t, h][:, c, :]
-                if (t, c) not in UNFUSED:
-                    nc.vector.tensor_tensor(out=into, in0=partner, in1=twin[t, c][:, cols], op=ALU.subtract)
-                    continue
-                if (t, c) in SCALAR_GATHERS:
-                    nc.scalar.activation(out=into, in_=partner, func=ACT.Copy)
-                else:
-                    nc.vector.tensor_copy(out=into, in_=partner)
-                nc.vector.tensor_tensor(out=into, in0=into, in1=coord[t, c][:, cols], op=ALU.subtract)
-            nc.scalar.activation(out=work[t, h][:], in_=work[t, h][:], func=ACT.Square)
-
-        def negate(t, h):
-            minus_ref[t, h] = ring.tile([P, D, P], F32, name="minus_ref")
-            into = minus_ref[t, h][:].rearrange("p d v -> p v d")
-            source = ref_sb[t][:, h * BANK : (h + 1) * BANK].rearrange("p (v d) -> p v d", d=D)
-            if NEG[t] == "A":
-                nc.scalar.activation(out=into, in_=source, func=ACT.Copy, scale=-16.0)
-            else:
-                nc.vector.tensor_scalar(into, source, -16.0, None, ALU.mult)
-
-        def distance(t, h):
-            square[t, h] = ring.tile([P, BANK], F32, name="square")
-            nc.vector.tensor_tensor(out=square[t, h][:], in0=work[t, h][:, 0, :], in1=work[t, h][:, 1, :], op=ALU.add)
-            dis = ring.tile([P, D, P], F32, name="dis")
-            nc.scalar.activation(
-                out=dis[:].rearrange("p d v -> p v d"), in_=square[t, h][:].rearrange("p (v d) -> p v d", d=D),
-                func=ACT.Sqrt, scale=256.0, bias=256.0 * 0.05,
-            )
-            signed = err_pool.tile([P, D, P], F32, name="signed")
-            for n, term in enumerate((minus_ref[t, h], dis)):
-                for d in range(D):
+        def turned_sum(role, terms):
+            bank = next_bank(role)
+            for n, term in enumerate(terms):
+                for b in range(BANK // P):
+                    block = slice(b * P, (b + 1) * P)
                     nc.tensor.matmul(
-                        out=signed[:, d, :], lhsT=term[:, d, :], rhs=ident[:], is_transpose=True,
-                        start=(n == 0 and d == 0), stop=(n == 1 and d == D - 1),
+                        out=bank[:, block], lhsT=term[:, block], rhs=ident[:], is_transpose=True,
+                        start=(n == 0 and b == 0), stop=(n == len(terms) - 1 and b == BANK // P - 1),
                     )
-            return signed
+            return bank[:]
 
-        def largest(t):
-            pairs = ring.tile([P, 2, 2, P], F32, name="pairs")
-            nc.vector.tensor_tensor(out=pairs[:], in0=err[t][:, :, 0:2, :], in1=err[t][:, :, 2:4, :], op=ALU.max)
-            nc.vector.tensor_tensor(out=worst[t][:], in0=pairs[:, :, 0, :], in1=pairs[:, :, 1, :], op=ALU.max)
-
-        units = [(t, h) for t in range(PACK) for h in range(2)]
-        signed = {}
-        for t in range(AHEAD):
-            project(t)
-        for n in range(len(units) + 2):
-            if n < len(units):
-                differences(*units[n])
-                t, h = units[n]
-                if h == 1 and t + AHEAD < PACK:
-                    project(t + AHEAD)
-            if 0 <= n < len(units) + 0:
-                negate(*units[n - 0])
-            if 1 <= n < len(units) + 1:
-                signed[units[n - 1]] = distance(*units[n - 1])
-            if n >= 2:
-                t, h = units[n - 2]
-                nc.scalar.activation(out=err[t][:, h, :, :], in_=signed[t, h][:], func=ACT.Abs)
-                if h == 1 and t < 8:
-                    largest(t)
-        for t in range(8, PACK):
-            largest(t)
-
-        shifts = square[LAST, 1][:, BANK - 2 :]
-        nc.gpsimd.memset(shifts[:, 0:1], -1.0)
-        nc.gpsimd.memset(shifts[:, 1:2], -2.5)
-
-        def score(t):
-            soft = held("soft%d" % t, [P, 2, 2, D, P], F32)
-            for part in ([slice(0, 1), slice(1, 2)] if t in HALVED else [slice(0, 2)]):
-                for s in range(2):
-                    nc.scalar.activation(
-                        out=soft[:, s, part, :, :], in_=err[t][:, part, :, :], func=ACT.Tanh,
-                        scale=0.125, bias=shifts[:, s : s + 1],
-                    )
-            total = sum_pool.tile([P, V], F32, name="total")
-            if t in HALVED:
-                order = [(n, h) for h in range(2) for n in range(2 * D + 1)]
-            else:
-                order = [(n, h) for n in range(2 * D + 1) for h in range(2)]
-            for n, h in order:
-                term = worst[t][:, h, :] if n == 0 else soft[:, (n - 1) // D, h, (n - 1) % D, :]
-                nc.tensor.matmul(
-                    out=total[:, h * P : (h + 1) * P], lhsT=term, rhs=ident[:],
-                    is_transpose=True, start=((n, h) == order[0]), stop=((n, h) == order[-1]),
-                )
-            value = err[t][:].rearrange("p h d v -> p (h d v)")[:, :V]
-            if QE[t] == "V":
-                nc.vector.tensor_scalar(
-                    value, total[:], unit_scale[:, t : t + 1], unit_bias[:, t : t + 1], ALU.mult, ALU.add
-                )
-            else:
-                nc.scalar.activation(
-                    out=value, in_=total[:], func=ACT.Identity,
-                    scale=unit_scale[:, t : t + 1], bias=unit_bias[:, t : t + 1],
-                )
-
-        slot_step = U // 2 // LANES
-
-        def look_up(t):
-            for h in range(2):
-                value = err[t][:].rearrange("p h d v -> p (h d v)").indirect(dom_sb[:, h * slot_step : (h + 1) * slot_step])
-                if DOM[2 * t + h] == "A":
-                    nc.scalar.activation(out=planes[h][:, t, :], in_=value, func=ACT.Copy)
-                else:
-                    nc.vector.tensor_copy(out=planes[h][:, t, :], in_=value)
-
-        for t in range(PACK):
-            score(t)
-        for t in range(PACK):
-            look_up(t)
-
-        for h in range(2):
-            hid = held("hid%d" % h, [P, U // 2, PACK], BF16)
-            codes = held("codes%d" % h, [P, U // 2], U32)
-            hid_plane = held("hid_plane%d" % h, [P, U // 2], U8)
-            result = held("result%d" % h, [P, U // 2], F32)
-            nc.vector.tensor_copy(
-                out=hid[:].rearrange("p (c i) t -> p c t i", i=4),
-                in_=planes[h][:].rearrange("p t (c i) -> p c t i", i=4),
-            )
-            nc.vector.quantize_mx(
-                out=codes[:].bitcast(FP8X4), scales=hid_plane[:], in_=hid[:].rearrange("p r t -> p (r t)")
-            )
-            acc = mm_pool.tile([P, BANK], F32, name="acc")
+        def project(t, c, h, role, copy, lo=0, hi=BANK):
+            acc = next_bank(role)
             nc.tensor.matmul_mx(
-                out=acc[:, : U // 2],
-                lhsT=w3_sb[:].bitcast(FP4X4),
-                lhsT_scale=w3_plane[:],
-                rhs=codes[:].bitcast(FP8X4),
-                rhs_scale=hid_plane[:],
+                out=acc[:, lo:hi],
+                lhsT=w_sb[c][:, 2 * P * t : 2 * P * (t + 1)].bitcast(FP4X4),
+                lhsT_scale=w_plane[c][:, P * t : P * (t + 1)],
+                rhs=xq_words[h][:, lo:hi].bitcast(FP8X4),
+                rhs_scale=xq_plane[h][:, lo:hi],
                 start=True,
                 stop=True,
             )
-            nc.scalar.copy(out=result[:], in_=acc[:, : U // 2])
-            nc.sync.dma_start(out=out[:, h * (U // 2) : (h + 1) * (U // 2)], in_=result[:])
+            copy(out=window[t, c][:, h * BANK + lo : h * BANK + hi], in_=acc[:, lo:hi])
+
+        def by_group(ap):
+            return ap.rearrange("p (v d) -> p v d", d=D)
+
+        def by_member(ap):
+            return ap.rearrange("p (d v) -> p v d", d=D)
+
+        def negate_ref(t):
+            for n in (2 * t, 2 * t + 1):
+                if n != LAST:
+                    cols = slice(PIECES[n][1] * BANK, (PIECES[n][1] + 1) * BANK)
+                    nc.vector.tensor_scalar(
+                        by_member(minus_ref[t][:, cols]), by_group(ref_sb[t][:, cols]), -1.0, None, ALU.mult
+                    )
+
+        def differ(n, c):
+            t, h = PIECES[n]
+            picks = entries(par_sb, h * BANK, (h + 1) * BANK)
+            partner = partners[n % 2][:, c, :]
+            own = window[t, c][:, h * BANK : (h + 1) * BANK]
+            by_scalar = c == 1 and n % 2 == 1
+            if on_tensor(n):
+                if by_scalar:
+                    nc.scalar.activation(out=partner, in_=window[t, c][:].indirect(picks), func=ACT.Copy, scale=-1.0)
+                else:
+                    nc.vector.tensor_scalar(partner, window[t, c][:].indirect(picks), -1.0, 0.0, ALU.mult, ALU.add)
+                difference[n, c] = turned_sum("difference", (own, partner))
+                return
+            if by_scalar:
+                nc.scalar.activation(out=partner, in_=window[t, c][:, :S].indirect(picks), func=ACT.Copy)
+            else:
+                nc.vector.tensor_copy(out=partner, in_=window[t, c][:, :S].indirect(picks))
+            nc.vector.tensor_tensor(out=partner, in0=partner, in1=own, op=ALU.subtract)
+            difference[n, c] = partner
+
+        def square(n):
+            both = squares[n % 2]
+            nc.scalar.activation(out=both[:, 0, :], in_=difference[n, 0], func=ACT.Square)
+            if n == LAST:
+                nc.vector.tensor_tensor(out=both[:, 1, :], in0=difference[n, 1], in1=difference[n, 1], op=ALU.mult)
+            else:
+                nc.scalar.activation(out=both[:, 1, :], in_=difference[n, 1], func=ACT.Square)
+            if on_tensor(n):
+                square_sum[n] = turned_sum("square", (both[:, 0, :], both[:, 1, :]))
+            else:
+                nc.vector.tensor_tensor(out=both[:, 0, :], in0=both[:, 0, :], in1=both[:, 1, :], op=ALU.add)
+                square_sum[n] = both[:, 0, :]
+
+        def compare(n):
+            t, h = PIECES[n]
+            dis = distances[n % 2][:]
+            cols = slice(h * BANK, (h + 1) * BANK)
+            if n == LAST:
+                nc.scalar.activation(out=dis, in_=square_sum[n], func=ACT.Sqrt, bias=0.05)
+                nc.vector.tensor_tensor(
+                    out=by_member(last_gap[:]), in0=by_group(dis), in1=by_group(ref_sb[t][:, cols]), op=ALU.subtract
+                )
+                signed[n] = turned_sum("signed", (last_gap[:],))
+                return
+            if on_tensor(n):
+                into = dis.rearrange("p (d v) -> p d v", d=D)
+                source = square_sum[n].rearrange("p (v d) -> p d v", d=D)
+            else:
+                into, source = by_member(dis), by_group(square_sum[n])
+            nc.scalar.activation(out=into, in_=source, func=ACT.Sqrt, bias=0.05)
+            signed[n] = turned_sum("signed", (minus_ref[t][:, cols], dis))
+
+        def error(n):
+            t, h = PIECES[n]
+            nc.scalar.activation(
+                out=err16[:, :, h, :, RUN * t : RUN * (t + 1)],
+                in_=signed[n].rearrange("p (d m r) -> p r d m", d=D, r=PACK), func=ACT.Abs, scale=float(2 * TERMS),
+            )
+
+        def largest(h):
+            err = err16[:, :, h, :, :]
+            nc.vector.tensor_tensor(out=pairs[h][:], in0=err[:, :, 0:2, :], in1=err[:, :, 2:4, :], op=ALU.max)
+            nc.vector.tensor_tensor(out=worst16[h][:], in0=pairs[h][:, :, 0, :], in1=pairs[h][:, :, 1, :], op=ALU.max)
+
+        for h in range(2):
+            for t in range(2):
+                for c in range(2):
+                    if (t, c) != (0, 0):
+                        project(t, c, h, "first", nc.scalar.copy)
+                    elif h == 0:
+                        project(t, c, h, "first", nc.vector.tensor_copy)
+                    else:
+                        for lo, hi in quarters:
+                            project(t, c, h, "first", nc.vector.tensor_copy, lo, hi)
+        for c in range(2):
+            for h in range(2):
+                project(2, c, h, "first", nc.scalar.copy)
+        negate_ref(0)
+
+        def project_last_tile(c, h):
+            by_vector = 2 * c + h >= 4 - VECTOR_COPIES
+            project(PACK - 1, c, h, "product", nc.vector.tensor_copy if by_vector else nc.scalar.copy)
+
+        for n in range(LAST + 4):
+            if n <= LAST:
+                differ(n, 0)
+                differ(n, 1)
+            if 1 <= n <= LAST + 1:
+                square(n - 1)
+            if n in (1, 2):
+                project_last_tile(n - 1, 0)
+            if 2 <= n <= LAST + 2:
+                compare(n - 2)
+            if n in (1, 2):
+                project_last_tile(n - 1, 1)
+            if n >= 3:
+                error(n - 3)
+            if n + 1 < PACK:
+                negate_ref(n + 1)
+            if n - 3 >= LAST - 1:
+                largest(PIECES[n - 3][1])
+
+        shifts = square_sum[LAST][:, 0:2]
+        nc.gpsimd.memset(shifts[:, 0:1], -1.0)
+        nc.gpsimd.memset(shifts[:, 1:2], -2.5)
+
+        soft = [held("soft%d" % r, [P, 2, 2, D * P], F32) for r in range(PACK)]
+        value = [tile[:].rearrange("p s h j -> p (s h j)") for tile in soft]
+
+        def score(r):
+            for h in range(2):
+                for s in range(2):
+                    nc.scalar.activation(
+                        out=soft[r][:, s, h, :], in_=err16[:, r, h, :, :].rearrange("p d m -> p (d m)"),
+                        func=ACT.Tanh, scale=0.125, bias=shifts[:, s : s + 1],
+                    )
+            terms = [(worst16[h][:, r, :], h) for h in range(2)]
+            for h in range(2):
+                pre_added = 2 * r + h < PRE_ADDED
+                if pre_added:
+                    first, second = soft[r][:, 0, h, :], soft[r][:, 1, h, :]
+                    nc.vector.tensor_tensor(out=first, in0=first, in1=second, op=ALU.add)
+                for s in range(1 if pre_added else 2):
+                    terms.extend((soft[r][:, s, h, d * P : (d + 1) * P], h) for d in range(D))
+            total = next_bank("score")
+            for n, (term, h) in enumerate(terms):
+                nc.tensor.matmul(
+                    out=total[:, h * P : (h + 1) * P], lhsT=term, rhs=ident[:],
+                    is_transpose=True, start=(n == 0), stop=(n == len(terms) - 1),
+                )
+            scale, bias = unit_scale[:, r : r + 1], unit_bias[:, r : r + 1]
+            if r in (0, PACK - 1):
+                nc.scalar.activation(out=value[r][:, :V], in_=total[:, :V], func=ACT.Identity, scale=scale, bias=bias)
+            else:
+                nc.vector.tensor_scalar(value[r][:, :V], total[:, :V], scale, bias, ALU.mult, ALU.add)
+
+        hid = held("hid", [P, U, PACK], BF16)
+        plain = held("plain", [P, U // 2], BF16)
+        codes = held("codes", [P, U], U32)
+        hid_plane = held("hid_plane", [P, U], U8)
+        result = held("result", [P, U], F32)
+        for r in range(PACK - 1):
+            score(r)
+            nc.vector.tensor_copy(out=hid[:, :, r], in_=value[r][:, : 2 * U].indirect(dom_sb[:]))
+
+        r = PACK - 1
+        score(r)
+        for lo in range(0, U, P):
+            picks = entries(dom_sb, lo, lo + P)
+            if lo < U // 2:
+                nc.vector.tensor_copy(out=hid[:, lo : lo + P, r], in_=value[r][:, :U].indirect(picks))
+            else:
+                into = plain[:, lo - U // 2 : lo - U // 2 + P]
+                nc.scalar.activation(out=into, in_=value[r].indirect(picks), func=ACT.Copy)
+        for h, copy in enumerate((nc.scalar.copy, nc.vector.tensor_copy)):
+            acc = next_bank("product")
+            for q in range(2):
+                lo = h * (U // 2) + q * P
+                slots = slice(lo, lo + P)
+                if h == 1:
+                    nc.vector.tensor_copy(out=hid[:, slots, r], in_=plain[:, q * P : (q + 1) * P])
+                nc.vector.quantize_mx(
+                    out=codes[:, slots].bitcast(FP8X4), scales=hid_plane[:, slots],
+                    in_=hid[:, slots, :].rearrange("p u r -> p (u r)"),
+                )
+                nc.tensor.matmul_mx(
+                    out=acc[:, q * P : (q + 1) * P],
+                    lhsT=w3_sb[:].bitcast(FP4X4),
+                    lhsT_scale=w3_plane[:],
+                    rhs=codes[:, slots].bitcast(FP8X4),
+                    rhs_scale=hid_plane[:, slots],
+                    start=True,
+                    stop=True,
+                )
+            half = slice(h * (U // 2), (h + 1) * (U // 2))
+            copy(out=result[:, half], in_=acc[:, : U // 2])
+            nc.sync.dma_start(out=out[:, half], in_=result[:, half])

@@ -130,7 +130,6 @@ def tile_picked_ylddts_worst_p_kernel(
         partners = [held("partner%d" % b, [P, 2, BANK], F32) for b in range(2)]
         squares = [held("square%d" % b, [P, 2, BANK], F32) for b in range(2)]
         distances = [held("distance%d" % b, [P, BANK], F32) for b in range(2)]
-        last_gap = held("last_gap", [P, BANK], F32)
         pairs = [held("pairs%d" % h, [P, PACK, 2, P], F32) for h in range(2)]
         difference, square_sum, signed = {}, {}, {}
 
@@ -165,12 +164,11 @@ def tile_picked_ylddts_worst_p_kernel(
             return ap.rearrange("p (d v) -> p v d", d=D)
 
         def negate_ref(t):
-            for n in (2 * t, 2 * t + 1):
-                if n != LAST:
-                    cols = slice(PIECES[n][1] * BANK, (PIECES[n][1] + 1) * BANK)
-                    nc.vector.tensor_scalar(
-                        by_member(minus_ref[t][:, cols]), by_group(ref_sb[t][:, cols]), -1.0, None, ALU.mult
-                    )
+            for h in range(2):
+                cols = slice(h * BANK, (h + 1) * BANK)
+                nc.vector.tensor_scalar(
+                    by_member(minus_ref[t][:, cols]), by_group(ref_sb[t][:, cols]), -1.0, None, ALU.mult
+                )
 
         def differ(n, c):
             t, h = PIECES[n]
@@ -195,7 +193,7 @@ def tile_picked_ylddts_worst_p_kernel(
         def square(n):
             both = squares[n % 2]
             nc.scalar.activation(out=both[:, 0, :], in_=difference[n, 0], func=ACT.Square)
-            if n == LAST:
+            if n >= LAST - 1:
                 nc.vector.tensor_tensor(out=both[:, 1, :], in0=difference[n, 1], in1=difference[n, 1], op=ALU.mult)
             else:
                 nc.scalar.activation(out=both[:, 1, :], in_=difference[n, 1], func=ACT.Square)
@@ -209,20 +207,17 @@ def tile_picked_ylddts_worst_p_kernel(
             t, h = PIECES[n]
             dis = distances[n % 2][:]
             cols = slice(h * BANK, (h + 1) * BANK)
-            if n == LAST:
-                nc.scalar.activation(out=dis, in_=square_sum[n], func=ACT.Sqrt, bias=0.05)
-                nc.vector.tensor_tensor(
-                    out=by_member(last_gap[:]), in0=by_group(dis), in1=by_group(ref_sb[t][:, cols]), op=ALU.subtract
-                )
-                signed[n] = turned_sum("signed", (last_gap[:],))
-                return
             if on_tensor(n):
                 into = dis.rearrange("p (d v) -> p d v", d=D)
                 source = square_sum[n].rearrange("p (v d) -> p d v", d=D)
             else:
                 into, source = by_member(dis), by_group(square_sum[n])
             nc.scalar.activation(out=into, in_=source, func=ACT.Sqrt, bias=0.05)
-            signed[n] = turned_sum("signed", (minus_ref[t][:, cols], dis))
+            if n == LAST:
+                nc.vector.tensor_tensor(out=dis, in0=dis, in1=minus_ref[t][:, cols], op=ALU.add)
+                signed[n] = turned_sum("signed", (dis,))
+            else:
+                signed[n] = turned_sum("signed", (minus_ref[t][:, cols], dis))
 
         def error(n):
             t, h = PIECES[n]
@@ -308,31 +303,32 @@ def tile_picked_ylddts_worst_p_kernel(
             else:
                 nc.vector.tensor_scalar(value[r][:, :V], total[:, :V], scale, bias, ALU.mult, ALU.add)
 
+        looked_up = held("looked_up", [P, PACK, U], BF16)
         hid = held("hid", [P, U, PACK], BF16)
-        plain = held("plain", [P, U // 2], BF16)
         codes = held("codes", [P, U], U32)
         hid_plane = held("hid_plane", [P, U], U8)
         result = held("result", [P, U], F32)
         for r in range(PACK - 1):
             score(r)
-            nc.vector.tensor_copy(out=hid[:, :, r], in_=value[r][:, : 2 * U].indirect(dom_sb[:]))
+            nc.vector.tensor_copy(out=looked_up[:, r, :], in_=value[r].indirect(dom_sb[:]))
 
-        r = PACK - 1
-        score(r)
+        score(PACK - 1)
         for lo in range(0, U, P):
-            picks = entries(dom_sb, lo, lo + P)
+            into = looked_up[:, PACK - 1, lo : lo + P]
+            source = value[PACK - 1].indirect(entries(dom_sb, lo, lo + P))
             if lo < U // 2:
-                nc.vector.tensor_copy(out=hid[:, lo : lo + P, r], in_=value[r][:, :U].indirect(picks))
+                nc.vector.tensor_copy(out=into, in_=source)
             else:
-                into = plain[:, lo - U // 2 : lo - U // 2 + P]
-                nc.scalar.activation(out=into, in_=value[r].indirect(picks), func=ACT.Copy)
+                nc.scalar.activation(out=into, in_=source, func=ACT.Copy)
         for h, copy in enumerate((nc.scalar.copy, nc.vector.tensor_copy)):
             acc = next_bank("product")
             for q in range(2):
                 lo = h * (U // 2) + q * P
                 slots = slice(lo, lo + P)
-                if h == 1:
-                    nc.vector.tensor_copy(out=hid[:, slots, r], in_=plain[:, q * P : (q + 1) * P])
+                nc.vector.tensor_copy(
+                    out=hid[:, slots, :].rearrange("p (g i) r -> p g r i", i=4),
+                    in_=looked_up[:, :, slots].rearrange("p r (g i) -> p g r i", i=4),
+                )
                 nc.vector.quantize_mx(
                     out=codes[:, slots].bitcast(FP8X4), scales=hid_plane[:, slots],
                     in_=hid[:, slots, :].rearrange("p u r -> p (u r)"),

from contextlib import ExitStack

import concourse.mybir as mybir
from concourse.masks import make_identity

K, T, S, D, N, H, V, U = 512, 2048, 1024, 4, 128, 512, 256, 512
FLOPS = 2 * (2 * K * H * S + H * N * U)

F32 = mybir.dt.float32
BF16 = mybir.dt.bfloat16
I32 = mybir.dt.int32
U32 = mybir.dt.uint32
U16 = mybir.dt.uint16
U8 = mybir.dt.uint8
FP8X4 = mybir.dt.float8_e4m3fn_x4
FP4X4 = mybir.dt.float4_e2m1fn_x4
ALU = mybir.AluOpType
ACT = mybir.ActivationFunctionType

P = 128
PACK = 4
BANK = 512
LANES = 16
RUN = P // PACK
TERMS = 2 * D
PIECES = [(t, h) for t in range(PACK) for h in range(2)]
LAST = len(PIECES) - 1
VECTOR_COPIES = 3
PRE_ADDED = 5


def load_scale_rows(nc, plane, scales):
    for q in range(4):
        nc.sync.dma_start(
            out=plane[32 * q : 32 * q + 4, :].bitcast(I32),
            in_=scales[0, 4 * q : 4 * q + 4, :].bitcast(I32),
        )


def on_tensor(n):
    return n % 2 == 1 and n != LAST


def tile_picked_ylddts_worst_p_kernel(
    tc, x_words, x_scales, w1_words, w1_scales, w2_words, w2_scales, ref, unit,
    w3_words, w3_scales, offs, par, dom, out,
):
    nc = tc.nc
    with ExitStack() as ctx:
        keep = ctx.enter_context(tc.tile_pool(name="keep", bufs=1))
        psum = ctx.enter_context(tc.psum_pool(name="psum", bufs=1))

        def held(name, shape, dtype):
            return keep.tile(shape, dtype, name=name, align_bytes=64)

        banks = [psum.tile([P, BANK], F32, name="bank%d" % b) for b in range(8)]
        roles = {
            "first": banks, "difference": banks[0:2], "product": banks[2:4], "square": banks[4:6],
            "signed": banks[6:8], "score": banks[0:4],
        }
        uses = {role: 0 for role in roles}

        def next_bank(role):
            uses[role] += 1
            return roles[role][(uses[role] - 1) % len(roles[role])]

        offs_sb = held("offs_sb", [P, S // LANES], U16)
        par_sb = held("par_sb", [P, S // LANES], U16)
        dom_sb = held("dom_sb", [P, U // LANES], U16)
        x_plane = held("x_plane", [P, T], U8)
        x_table = held("x_table", [P, T], I32)
        w_sb = [held("w_sb%d" % c, [P, 2 * H], U8) for c in range(2)]
        w_plane = [held("w_plane%d" % c, [P, H], U8) for c in range(2)]
        ident = held("ident", [P, P], F32)

        window = {(t, c): held("window%d_%d" % (t, c), [P, 2 * S], F32) for t in range(PACK) for c in range(2)}
        ref_sb = [window[t // 2, t % 2][:, S:] for t in range(PACK)]
        minus_ref = [window[2 + t // 2, t % 2][:, S:] for t in range(PACK)]

        def load_ref(t):
            nc.sync.dma_start(out=ref_sb[t], in_=ref[P * t : P * (t + 1), :])

        nc.gpsimd.memset(x_plane[:, : T // 2].bitcast(I32), 0)
        nc.vector.memset(x_plane[:, T // 2 :].bitcast(I32), 0)
        for plane in w_plane:
            nc.vector.memset(plane[:].bitcast(I32), 0)

        nc.sync.dma_start(out=offs_sb[:], in_=offs)
        nc.sync.dma_start(out=par_sb[:], in_=par)
        load_scale_rows(nc, x_plane[:], x_scales)
        nc.sync.dma_start(out=x_table[:], in_=x_words[0].rearrange("p n r -> p (n r)").bitcast(I32))
        nc.gpsimd.dma_start(out=w_sb[0][:].bitcast(I32), in_=w1_words[0].bitcast(I32))
        nc.gpsimd.dma_start(out=w_sb[1][:].bitcast(I32), in_=w2_words[0].bitcast(I32))
        load_ref(0)
        load_scale_rows(nc, w_plane[0][:], w1_scales)
        load_scale_rows(nc, w_plane[1][:], w2_scales)
        for t in range(1, PACK):
            load_ref(t)
        nc.sync.dma_start(out=dom_sb[:], in_=dom)
        make_identity(nc, ident[:])
        unit_sb = held("unit_sb", [P, PACK], F32)
        w3_sb = held("w3_sb", [P, 2 * N], U8)
        w3_plane = held("w3_plane", [P, N], U8)
        nc.vector.memset(w3_plane[:].bitcast(I32), 0)
        nc.sync.dma_start(out=unit_sb[:], in_=unit.rearrange("(p r) o -> p (r o)", r=PACK))
        nc.sync.dma_start(out=w3_sb[:].bitcast(I32), in_=w3_words[0].bitcast(I32))
        load_scale_rows(nc, w3_plane[:], w3_scales)

        def entries(list_sb, lo, hi):
            return list_sb[:, lo // LANES : hi // LANES]

        xq_plane = [held("xq_plane%d" % h, [P, BANK], U8) for h in range(2)]
        xq_words = [held("xq_words%d" % h, [P, BANK], U32) for h in range(2)]
        quarters = ((0, BANK // 2), (BANK // 2, BANK))
        for h in range(2):
            picks = entries(offs_sb, h * BANK, (h + 1) * BANK)
            nc.vector.tensor_copy(out=xq_plane[h][:], in_=x_plane[:].indirect(picks))
        words = x_table[:].bitcast(U32)
        nc.vector.tensor_copy(out=xq_words[0][:], in_=words.indirect(entries(offs_sb, 0, BANK)))
        for lo, hi in quarters:
            nc.vector.tensor_copy(out=xq_words[1][:, lo:hi], in_=words.indirect(entries(offs_sb, BANK + lo, BANK + hi)))

        unit_scale = held("unit_scale", [P, PACK], F32)
        unit_bias = held("unit_bias", [P, PACK], F32)
        nc.gpsimd.tensor_scalar(unit_scale[:], unit_sb[:], -1.0 / (2 * TERMS), 0.0, ALU.mult, ALU.add)
        nc.gpsimd.tensor_scalar(unit_bias[:], unit_sb[:], 0.5, 0.0, ALU.mult, ALU.add)

        err16 = held("err16", [P, PACK, 2, D, P], F32)
        worst16 = [held("worst16_%d" % h, [P, PACK, P], F32) for h in range(2)]
        partners = [held("partner%d" % b, [P, 2, BANK], F32) for b in range(2)]
        squares = [held("square%d" % b, [P, 2, BANK], F32) for b in range(2)]
        distances = [held("distance%d" % b, [P, BANK], F32) for b in range(2)]
        pairs = [held("pairs%d" % h, [P, PACK, 2, P], F32) for h in range(2)]
        difference, square_sum, signed = {}, {}, {}

        def turned_sum(role, terms):
            bank = next_bank(role)
            for n, term in enumerate(terms):
                for b in range(BANK // P):
                    block = slice(b * P, (b + 1) * P)
                    nc.tensor.matmul(
                        out=bank[:, block], lhsT=term[:, block], rhs=ident[:], is_transpose=True,
                        start=(n == 0 and b == 0), stop=(n == len(terms) - 1 and b == BANK // P - 1),
                    )
            return bank[:]

        def project(t, c, h, role, copy, lo=0, hi=BANK):
            acc = next_bank(role)
            nc.tensor.matmul_mx(
                out=acc[:, lo:hi],
                lhsT=w_sb[c][:, 2 * P * t : 2 * P * (t + 1)].bitcast(FP4X4),
                lhsT_scale=w_plane[c][:, P * t : P * (t + 1)],
                rhs=xq_words[h][:, lo:hi].bitcast(FP8X4),
                rhs_scale=xq_plane[h][:, lo:hi],
                start=True,
                stop=True,
            )
            copy(out=window[t, c][:, h * BANK + lo : h * BANK + hi], in_=acc[:, lo:hi])

        def by_group(ap):
            return ap.rearrange("p (v d) -> p v d", d=D)

        def by_member(ap):
            return ap.rearrange("p (d v) -> p v d", d=D)

        def negate_ref(t):
            for h in range(2):
                cols = slice(h * BANK, (h + 1) * BANK)
                nc.vector.tensor_scalar(
                    by_member(minus_ref[t][:, cols]), by_group(ref_sb[t][:, cols]), -1.0, None, ALU.mult
                )

        def differ(n, c):
            t, h = PIECES[n]
            picks = entries(par_sb, h * BANK, (h + 1) * BANK)
            partner = partners[n % 2][:, c, :]
            own = window[t, c][:, h * BANK : (h + 1) * BANK]
            by_scalar = c == 1 and n % 2 == 1
            if on_tensor(n):
                if by_scalar:
                    nc.scalar.activation(out=partner, in_=window[t, c][:].indirect(picks), func=ACT.Copy, scale=-1.0)
                else:
                    nc.vector.tensor_scalar(partner, window[t, c][:].indirect(picks), -1.0, 0.0, ALU.mult, ALU.add)
                difference[n, c] = turned_sum("difference", (own, partner))
                return
            if by_scalar:
                nc.scalar.activation(out=partner, in_=window[t, c][:, :S].indirect(picks), func=ACT.Copy)
            else:
                nc.vector.tensor_copy(out=partner, in_=window[t, c][:, :S].indirect(picks))
            nc.vector.tensor_tensor(out=partner, in0=partner, in1=own, op=ALU.subtract)
            difference[n, c] = partner

        def square(n):
            both = squares[n % 2]
            nc.scalar.activation(out=both[:, 0, :], in_=difference[n, 0], func=ACT.Square)
            if n >= LAST - 1:
                nc.vector.tensor_tensor(out=both[:, 1, :], in0=difference[n, 1], in1=difference[n, 1], op=ALU.mult)
            else:
                nc.scalar.activation(out=both[:, 1, :], in_=difference[n, 1], func=ACT.Square)
            if on_tensor(n):
                square_sum[n] = turned_sum("square", (both[:, 0, :], both[:, 1, :]))
            else:
                nc.vector.tensor_tensor(out=both[:, 0, :], in0=both[:, 0, :], in1=both[:, 1, :], op=ALU.add)
                square_sum[n] = both[:, 0, :]

        def compare(n):
            t, h = PIECES[n]
            dis = distances[n % 2][:]
            cols = slice(h * BANK, (h + 1) * BANK)
            if on_tensor(n):
                into = dis.rearrange("p (d v) -> p d v", d=D)
                source = square_sum[n].rearrange("p (v d) -> p d v", d=D)
            else:
                into, source = by_member(dis), by_group(square_sum[n])
            nc.scalar.activation(out=into, in_=source, func=ACT.Sqrt, bias=0.05)
            if n == LAST:
                nc.vector.tensor_tensor(out=dis, in0=dis, in1=minus_ref[t][:, cols], op=ALU.add)
                signed[n] = turned_sum("signed", (dis,))
            else:
                signed[n] = turned_sum("signed", (minus_ref[t][:, cols], dis))

        def error(n):
            t, h = PIECES[n]
            nc.scalar.activation(
                out=err16[:, :, h, :, RUN * t : RUN * (t + 1)],
                in_=signed[n].rearrange("p (d m r) -> p r d m", d=D, r=PACK), func=ACT.Abs, scale=float(2 * TERMS),
            )

        def largest(h):
            err = err16[:, :, h, :, :]
            nc.vector.tensor_tensor(out=pairs[h][:], in0=err[:, :, 0:2, :], in1=err[:, :, 2:4, :], op=ALU.max)
            nc.vector.tensor_tensor(out=worst16[h][:], in0=pairs[h][:, :, 0, :], in1=pairs[h][:, :, 1, :], op=ALU.max)

        for h in range(2):
            for t in range(2):
                for c in range(2):
                    if (t, c) != (0, 0):
                        project(t, c, h, "first", nc.scalar.copy)
                    elif h == 0:
                        project(t, c, h, "first", nc.vector.tensor_copy)
                    else:
                        for lo, hi in quarters:
                            project(t, c, h, "first", nc.vector.tensor_copy, lo, hi)
        for c in range(2):
            for h in range(2):
                project(2, c, h, "first", nc.scalar.copy)
        negate_ref(0)

        def project_last_tile(c, h):
            by_vector = 2 * c + h >= 4 - VECTOR_COPIES
            project(PACK - 1, c, h, "product", nc.vector.tensor_copy if by_vector else nc.scalar.copy)

        for n in range(LAST + 4):
            if n <= LAST:
                differ(n, 0)
                differ(n, 1)
            if 1 <= n <= LAST + 1:
                square(n - 1)
            if n in (1, 2):
                project_last_tile(n - 1, 0)
            if 2 <= n <= LAST + 2:
                compare(n - 2)
            if n in (1, 2):
                project_last_tile(n - 1, 1)
            if n >= 3:
                error(n - 3)
            if n + 1 < PACK:
                negate_ref(n + 1)
            if n - 3 >= LAST - 1:
                largest(PIECES[n - 3][1])

        shifts = square_sum[LAST][:, 0:2]
        nc.gpsimd.memset(shifts[:, 0:1], -1.0)
        nc.gpsimd.memset(shifts[:, 1:2], -2.5)

        soft = [held("soft%d" % r, [P, 2, 2, D * P], F32) for r in range(PACK)]
        value = [tile[:].rearrange("p s h j -> p (s h j)") for tile in soft]

        def score(r):
            for h in range(2):
                for s in range(2):
                    nc.scalar.activation(
                        out=soft[r][:, s, h, :], in_=err16[:, r, h, :, :].rearrange("p d m -> p (d m)"),
                        func=ACT.Tanh, scale=0.125, bias=shifts[:, s : s + 1],
                    )
            terms = [(worst16[h][:, r, :], h) for h in range(2)]
            for h in range(2):
                pre_added = 2 * r + h < PRE_ADDED
                if pre_added:
                    first, second = soft[r][:, 0, h, :], soft[r][:, 1, h, :]
                    nc.vector.tensor_tensor(out=first, in0=first, in1=second, op=ALU.add)
                for s in range(1 if pre_added else 2):
                    terms.extend((soft[r][:, s, h, d * P : (d + 1) * P], h) for d in range(D))
            total = next_bank("score")
            for n, (term, h) in enumerate(terms):
                nc.tensor.matmul(
                    out=total[:, h * P : (h + 1) * P], lhsT=term, rhs=ident[:],
                    is_transpose=True, start=(n == 0), stop=(n == len(terms) - 1),
                )
            scale, bias = unit_scale[:, r : r + 1], unit_bias[:, r : r + 1]
            if r in (0, PACK - 1):
                nc.scalar.activation(out=value[r][:, :V], in_=total[:, :V], func=ACT.Identity, scale=scale, bias=bias)
            else:
                nc.vector.tensor_scalar(value[r][:, :V], total[:, :V], scale, bias, ALU.mult, ALU.add)

        looked_up = held("looked_up", [P, PACK, U], BF16)
        hid = held("hid", [P, U, PACK], BF16)
        codes = held("codes", [P, U], U32)
        hid_plane = held("hid_plane", [P, U], U8)
        result = held("result", [P, U], F32)
        for r in range(PACK - 1):
            score(r)
            nc.vector.tensor_copy(out=looked_up[:, r, :], in_=value[r].indirect(dom_sb[:]))

        score(PACK - 1)
        for lo in range(0, U, P):
            into = looked_up[:, PACK - 1, lo : lo + P]
            source = value[PACK - 1].indirect(entries(dom_sb, lo, lo + P))
            if lo < U // 2:
                nc.vector.tensor_copy(out=into, in_=source)
            else:
                nc.scalar.activation(out=into, in_=source, func=ACT.Copy)
        for h, copy in enumerate((nc.scalar.copy, nc.vector.tensor_copy)):
            acc = next_bank("product")
            for q in range(2):
                lo = h * (U // 2) + q * P
                slots = slice(lo, lo + P)
                nc.vector.tensor_copy(
                    out=hid[:, slots, :].rearrange("p (g i) r -> p g r i", i=4),
                    in_=looked_up[:, :, slots].rearrange("p r (g i) -> p g r i", i=4),
                )
                nc.vector.quantize_mx(
                    out=codes[:, slots].bitcast(FP8X4), scales=hid_plane[:, slots],
                    in_=hid[:, slots, :].rearrange("p u r -> p (u r)"),
                )
                nc.tensor.matmul_mx(
                    out=acc[:, q * P : (q + 1) * P],
                    lhsT=w3_sb[:].bitcast(FP4X4),
                    lhsT_scale=w3_plane[:],
                    rhs=codes[:, slots].bitcast(FP8X4),
                    rhs_scale=hid_plane[:, slots],
                    start=True,
                    stop=True,
                )
            half = slice(h * (U // 2), (h + 1) * (U // 2))
            copy(out=result[:, half], in_=acc[:, : U // 2])
            nc.sync.dma_start(out=out[:, half], in_=result[:, half])
